import numpy as np
CORES = [3,0,2,1,6,7,4,5]
N = 8
def setup_inputs(rng):
    return {"x": rng.standard_normal((N, 128, 16384), dtype=np.float32)}
def reference(x):
    s = x.sum(axis=0, dtype=np.float64).astype(x.dtype)
    return {"y": np.broadcast_to(s, (N,) + s.shape)}

@@ -1,0 +1,60 @@
+from concourse.bass import DstId, RemoteDMATransfer
+from concourse.mybir import AluOpType
+
+Q = 4
+W = 4096
+ALL = 0xFFFF
+
+SCRATCH = {
+    "xs": ("dram", [Q, 128, W], "float32"),
+    "land": ("dram", [Q, 128, W], "float32"),
+    "part": ("dram", [128, W], "float32"),
+    "res": ("dram", [Q, 128, W], "float32"),
+}
+SEMAPHORES = ["loaded", "acc", "stored", "sent", "arr1", "arr2", "arr3"]
+
+
+def rank_program(g, core, T, topo):
+    if T.rank_of(core) is None:
+        return
+    s = T.sem
+    mine = sorted(c for c in T.cores if topo.die(c) == topo.die(core))
+    other = sorted(c for c in T.cores if topo.die(c) != topo.die(core))
+    m = mine.index(core)
+    partner = other[m]
+    mates = [(k, c) for k, c in enumerate(mine) if c != core]
+    rows = 128 // Q
+
+    def dst(c):
+        rid, pid, _se = topo.addr(c)
+        return DstId(rid=rid, pnc=pid)
+
+    g.dma_start(T.xs[:], T.x[:]).then_inc(s.loaded, 16)
+    g.dma_start(T.res[m], T.x[m * rows:(m + 1) * rows, :]).then_inc(s.acc, 16)
+    g.wait_ge(s.loaded, 16)
+
+    for k, c in mates:
+        rid, pid, _se = topo.addr(c)
+        g.remote_dma(T.land[m], T.xs[k], s.arr1, s.sent, pid, rid, ALL)
+    g.wait_ge(s.arr1, 16 * len(mates))
+    pieces = [T.xs[m]] + [T.land[k] for k, _c in mates]
+
+    g.remote_dma_fused([RemoteDMATransfer(dst_ids=[dst(partner)], dma_engine_mask=ALL, remote_sem=s.arr2,
+                                          srcs=pieces, dsts=[T.part[:]], alu_op=1)], local_sem=s.sent)
+    g.wait_ge(s.arr2, 16)
+
+    g.remote_dma_fused([RemoteDMATransfer(dst_ids=[dst(c) for _k, c in mates], dma_engine_mask=ALL,
+                                          remote_sem=s.arr3, srcs=pieces + [T.part[:]],
+                                          dsts=[T.res[m] for _ in mates], alu_op=1)], local_sem=s.sent)
+
+    n = 16
+    for src in pieces[1:] + [T.part[:]]:
+        g.wait_ge(s.acc, n)
+        g.dma_start(T.res[m], src, accum_op=AluOpType.add, max_dma_last_dim=8192).then_inc(s.acc, 16)
+        n += 16
+    g.wait_ge(s.acc, n)
+
+    g.wait_ge(s.arr3, 16 * len(mates))
+    g.dma_start(T.y[:], T.res[:]).then_inc(s.stored, 16)
+    g.wait_ge(s.stored, 16)
+    g.wait_ge(s.sent, 16 * (len(mates) + 2))

@@ -3,15 +3,17 @@ from concourse.mybir import AluOpType
 
 Q = 4
 W = 4096
+ROWS = 128 // Q
 ALL = 0xFFFF
 
 SCRATCH = {
     "xs": ("dram", [Q, 128, W], "float32"),
     "land": ("dram", [Q, 128, W], "float32"),
     "part": ("dram", [128, W], "float32"),
+    "side": ("dram", [128, W], "float32"),
     "res": ("dram", [Q, 128, W], "float32"),
 }
-SEMAPHORES = ["loaded", "acc", "stored", "sent", "arr1", "arr2", "arr3"]
+SEMAPHORES = ["loaded", "acc_a", "acc_b", "stored", "sent", "arr1", "arr2", "arr3"]
 
 
 def rank_program(g, core, T, topo):
@@ -23,38 +25,51 @@ def rank_program(g, core, T, topo):
     m = mine.index(core)
     partner = other[m]
     mates = [(k, c) for k, c in enumerate(mine) if c != core]
-    rows = 128 // Q
+    y_m = T.y[m * ROWS:(m + 1) * ROWS, :]
 
     def dst(c):
         rid, pid, _se = topo.addr(c)
         return DstId(rid=rid, pnc=pid)
 
+    def add(out, in_, sem):
+        g.dma_start(out, in_, accum_op=AluOpType.add, max_dma_last_dim=8192).then_inc(sem, 16)
+
     g.dma_start(T.xs[:], T.x[:]).then_inc(s.loaded, 16)
-    g.dma_start(T.res[m], T.x[m * rows:(m + 1) * rows, :]).then_inc(s.acc, 16)
+    g.dma_start(y_m, T.x[m * ROWS:(m + 1) * ROWS, :]).then_inc(s.acc_a, 16)
     g.wait_ge(s.loaded, 16)
 
     for k, c in mates:
         rid, pid, _se = topo.addr(c)
         g.remote_dma(T.land[m], T.xs[k], s.arr1, s.sent, pid, rid, ALL)
     g.wait_ge(s.arr1, 16 * len(mates))
-    pieces = [T.xs[m]] + [T.land[k] for k, _c in mates]
+    got = [T.land[k] for k, _c in mates]
+    pieces = [T.xs[m]] + got
 
     g.remote_dma_fused([RemoteDMATransfer(dst_ids=[dst(partner)], dma_engine_mask=ALL, remote_sem=s.arr2,
                                           srcs=pieces, dsts=[T.part[:]], alu_op=1)], local_sem=s.sent)
-    g.wait_ge(s.arr2, 16)
 
+    g.wait_ge(s.acc_a, 16)
+    add(y_m, got[0], s.acc_a)
+    g.dma_start(T.side[:], got[2]).then_inc(s.acc_b, 16)
+    g.wait_ge(s.acc_a, 32)
+    add(y_m, got[1], s.acc_a)
+
+    g.wait_ge(s.arr2, 16)
     g.remote_dma_fused([RemoteDMATransfer(dst_ids=[dst(c) for _k, c in mates], dma_engine_mask=ALL,
                                           remote_sem=s.arr3, srcs=pieces + [T.part[:]],
                                           dsts=[T.res[m] for _ in mates], alu_op=1)], local_sem=s.sent)
 
-    n = 16
-    for src in pieces[1:] + [T.part[:]]:
-        g.wait_ge(s.acc, n)
-        g.dma_start(T.res[m], src, accum_op=AluOpType.add, max_dma_last_dim=8192).then_inc(s.acc, 16)
-        n += 16
-    g.wait_ge(s.acc, n)
+    g.wait_ge(s.acc_b, 16)
+    add(T.side[:], T.part[:], s.acc_b)
+    g.wait_ge(s.acc_a, 48)
+    g.wait_ge(s.acc_b, 32)
+    add(y_m, T.side[:], s.acc_a)
 
     g.wait_ge(s.arr3, 16 * len(mates))
-    g.dma_start(T.y[:], T.res[:]).then_inc(s.stored, 16)
-    g.wait_ge(s.stored, 16)
+    runs = [(lo, hi) for lo, hi in ((0, m), (m + 1, Q)) if lo < hi]
+    for lo, hi in runs:
+        g.dma_start(T.y[lo * ROWS:hi * ROWS, :], T.res[lo:hi]).then_inc(s.stored, 16)
+
+    g.wait_ge(s.acc_a, 64)
+    g.wait_ge(s.stored, 16 * len(runs))
     g.wait_ge(s.sent, 16 * (len(mates) + 2))

from concourse.bass import DstId, RemoteDMATransfer
from concourse.mybir import AluOpType

Q = 4
W = 4096
ROWS = 128 // Q
ALL = 0xFFFF

SCRATCH = {
    "xs": ("dram", [Q, 128, W], "float32"),
    "land": ("dram", [Q, 128, W], "float32"),
    "part": ("dram", [128, W], "float32"),
    "side": ("dram", [128, W], "float32"),
    "res": ("dram", [Q, 128, W], "float32"),
}
SEMAPHORES = ["loaded", "acc_a", "acc_b", "stored", "sent", "arr1", "arr2", "arr3"]


def rank_program(g, core, T, topo):
    if T.rank_of(core) is None:
        return
    s = T.sem
    mine = sorted(c for c in T.cores if topo.die(c) == topo.die(core))
    other = sorted(c for c in T.cores if topo.die(c) != topo.die(core))
    m = mine.index(core)
    partner = other[m]
    mates = [(k, c) for k, c in enumerate(mine) if c != core]
    y_m = T.y[m * ROWS:(m + 1) * ROWS, :]

    def dst(c):
        rid, pid, _se = topo.addr(c)
        return DstId(rid=rid, pnc=pid)

    def add(out, in_, sem):
        g.dma_start(out, in_, accum_op=AluOpType.add, max_dma_last_dim=8192).then_inc(sem, 16)

    g.dma_start(T.xs[:], T.x[:]).then_inc(s.loaded, 16)
    g.dma_start(y_m, T.x[m * ROWS:(m + 1) * ROWS, :]).then_inc(s.acc_a, 16)
    g.wait_ge(s.loaded, 16)

    for k, c in mates:
        rid, pid, _se = topo.addr(c)
        g.remote_dma(T.land[m], T.xs[k], s.arr1, s.sent, pid, rid, ALL)
    g.wait_ge(s.arr1, 16 * len(mates))
    got = [T.land[k] for k, _c in mates]
    pieces = [T.xs[m]] + got

    g.remote_dma_fused([RemoteDMATransfer(dst_ids=[dst(partner)], dma_engine_mask=ALL, remote_sem=s.arr2,
                                          srcs=pieces, dsts=[T.part[:]], alu_op=1)], local_sem=s.sent)

    g.wait_ge(s.acc_a, 16)
    add(y_m, got[0], s.acc_a)
    g.dma_start(T.side[:], got[2]).then_inc(s.acc_b, 16)
    g.wait_ge(s.acc_a, 32)
    add(y_m, got[1], s.acc_a)

    g.wait_ge(s.arr2, 16)
    g.remote_dma_fused([RemoteDMATransfer(dst_ids=[dst(c) for _k, c in mates], dma_engine_mask=ALL,
                                          remote_sem=s.arr3, srcs=pieces + [T.part[:]],
                                          dsts=[T.res[m] for _ in mates], alu_op=1)], local_sem=s.sent)

    g.wait_ge(s.acc_b, 16)
    add(T.side[:], T.part[:], s.acc_b)
    g.wait_ge(s.acc_a, 48)
    g.wait_ge(s.acc_b, 32)
    add(y_m, T.side[:], s.acc_a)

    g.wait_ge(s.arr3, 16 * len(mates))
    runs = [(lo, hi) for lo, hi in ((0, m), (m + 1, Q)) if lo < hi]
    for lo, hi in runs:
        g.dma_start(T.y[lo * ROWS:hi * ROWS, :], T.res[lo:hi]).then_inc(s.stored, 16)

    g.wait_ge(s.acc_a, 64)
    g.wait_ge(s.stored, 16 * len(runs))
    g.wait_ge(s.sent, 16 * (len(mates) + 2))
